import numpy as np
import ml_dtypes


def mxq(x, axis, fmt="e4m3"):
    dtype, down = {"e4m3": (ml_dtypes.float8_e4m3fn, 7), "e5m2": (ml_dtypes.float8_e5m2, 14)}[fmt]
    v = np.moveaxis(np.asarray(x, np.float32).astype(ml_dtypes.bfloat16).astype(np.float64), axis, -1)
    blocks = v.reshape(v.shape[:-1] + (-1, 32))
    amax = np.abs(blocks).max(-1, keepdims=True)
    byte = np.maximum(np.where(amax > 0, np.frexp(amax)[1] - 1 + 127, 0) - down, 1)
    scale = np.exp2(byte - 127.0)
    codes = (blocks / scale).astype(np.float32).astype(dtype).astype(np.float64)
    return np.moveaxis((codes * scale).reshape(v.shape), -1, axis)


WIDE = False


def mx_kscale(k):
    if not WIDE:
        return np.ones(k)
    levels = np.array([10, -10, 5, -5, 0])
    if k % 512:
        return np.exp2(np.random.permutation(np.resize(levels, k // 32))).repeat(32)
    a = np.empty((k // 512, 16))
    for p in range(k // 512):
        a[p, :8] = np.random.permutation(np.resize(levels, 8))
        for g in range(8):
            far = levels[np.abs(levels - a[p, g]) >= 10]
            a[p, g + 8] = far[np.random.randint(len(far))]
    return np.exp2(a.ravel()).repeat(32)


def f64(x):
    return np.asarray(x).astype(np.float64)


def striped(idx):
    return np.tile(idx.reshape(-1, 16).T, (8, 1)).astype(np.uint16)


def unstriped(offs):
    return offs[:16].T.reshape(-1).astype(np.int64)


def pack_weight(w):
    k, n = w.shape
    w = f64(np.asarray(w, np.float32).astype(ml_dtypes.bfloat16)).reshape(k // 32, 32, n)
    amax = np.abs(w).max(1)
    byte = np.clip(np.where(amax > 0, np.frexp(amax)[1] - 1 + 127 - 7, 1), 1, 254)
    scaled = (w * np.exp2(127.0 - byte)[:, None, :]).reshape(k, n).astype(np.float32)
    words = np.ascontiguousarray(scaled.reshape(k // 512, 128, 4, n).transpose(0, 1, 3, 2)).astype(ml_dtypes.float8_e4m3fn).view(np.uint8)
    return words, np.ascontiguousarray(byte.astype(np.uint8).reshape(k // 512, 16, n))


def unpack_weight(words, scales):
    g, p, n, _ = words.shape
    vals = np.ascontiguousarray(words).view(ml_dtypes.float8_e4m3fn).astype(np.float64) * np.repeat(np.exp2(scales.astype(np.float64) - 127.0), 8, axis=1)[..., None]
    return vals.transpose(0, 1, 3, 2).reshape(g * 512, n)


K, T, S, D, N, H = 512, 2048, 512, 4, 256, 512


def setup_inputs():
    n = np.random.standard_normal
    s = mx_kscale(K)[:, None]
    u = mx_kscale(H)
    packed_xT = pack_weight(n((K, T)) * s)
    return {
        "x_words": packed_xT[0],
        "x_scales": packed_xT[1],
        "w1": (n((K, H)) / np.sqrt(K) / s).astype(np.float32),
        "w2": (n((K, H)) / np.sqrt(K) / s).astype(np.float32),
        "meas": (n((H, S))).astype(np.float32),
        "unit": (np.random.uniform(0.6, 1.4, (H, 1)) * u[:, None]).astype(np.float32),
        "w3": (n((H, N)) / np.sqrt(H) / u[:, None]).astype(np.float32),
        "offs": striped(np.random.permutation(T)[:S]),
        "brn": striped(np.random.permutation(S)),
    }


def reference(x_words, x_scales, w1, w2, meas, unit, w3, offs, brn):
    xq = unpack_weight(x_words, x_scales)[:, unstriped(offs)]
    wg = mxq(f64(w2), 0, "e4m3").T @ xq
    wei = np.log(np.exp(wg) + 1.0)
    mu = mxq(f64(w1), 0, "e4m3").T @ xq
    lik = np.exp(-1.5 * ((np.tanh(f64(meas) - mu)) ** 2))
    num = wei * lik
    den = num.reshape(len(num), -1, D).sum(axis=2) + 0.3
    upd = num / np.repeat(den, D, axis=1)
    mix = 0.2 * wei + 0.8 * upd
    ub = upd[:, unstriped(brn)]
    hid = f64(unit) * (mix * (mu + 0.7 * ub))
    return mxq(f64(w3), 0, "e4m3").T @ mxq(hid, 0, "e4m3")

@@ -1,0 +1,225 @@
+from contextlib import ExitStack
+
+import concourse.mybir as mybir
+from concourse.masks import make_identity
+
+K, T, S, D, N, H = 512, 2048, 512, 4, 256, 512
+FLOPS = 2 * K * H * S * 2 + 2 * H * N * S
+
+F32 = mybir.dt.float32
+BF16 = mybir.dt.bfloat16
+I32 = mybir.dt.int32
+U32 = mybir.dt.uint32
+U16 = mybir.dt.uint16
+U8 = mybir.dt.uint8
+FP8X4 = mybir.dt.float8_e4m3fn_x4
+ALU = mybir.AluOpType
+ACT = mybir.ActivationFunctionType
+
+P = 128
+PACK = 4
+HALF = S // 2
+GROUPS = S // D
+LN_FLOOR = 2.0**-60
+
+
+def tile_picked_ygmphd_mean_p_kernel(tc, x_words, x_scales, w1, w2, meas, unit, w3, offs, brn, out):
+    nc = tc.nc
+    with ExitStack() as ctx:
+        sb = ctx.enter_context(tc.tile_pool(name="sb", bufs=1))
+        ps = ctx.enter_context(tc.psum_pool(name="ps", bufs=1))
+
+        def tile(shape, dtype, name):
+            return sb.tile(shape, dtype, name=name, align_bytes=64)
+
+        def bank(name, tag):
+            return ps.tile([P, S], F32, name=name, tag=tag)
+
+        offs_sb = sb.tile([P, S // 16], U16, name="offs_sb")
+        nc.sync.dma_start(offs_sb[:], offs)
+        xs_table = tile([P, T], U8, "xs_table")
+        nc.vector.memset(xs_table[:].bitcast(I32), 0)
+        xw_table = tile([P, T], U32, "xw_table")
+        nc.sync.dma_start(xw_table[:].bitcast(I32), x_words[0].rearrange("p n r -> p (n r)").bitcast(I32))
+        for q in range(4):
+            nc.sync.dma_start(
+                xs_table[32 * q : 32 * q + 4, :].bitcast(I32), x_scales[0, 4 * q : 4 * q + 4, :].bitcast(I32)
+            )
+
+        def load_halves(w, name):
+            halves = []
+            for h in range(2):
+                raw = tile([P, PACK, H // 2], F32, "%s_raw%d" % (name, h))
+                nc.sync.dma_start(raw[:], w.rearrange("(p j) c -> p j c", j=PACK)[:, :, h * (H // 2) : (h + 1) * (H // 2)])
+                halves.append(raw)
+            return halves
+
+        w2_raw = load_halves(w2, "w2")
+        w1_raw = load_halves(w1, "w1")
+        meas_sb = []
+        for t in range(PACK):
+            m_t = tile([P, S], F32, "meas%d" % t)
+            nc.sync.dma_start(m_t[:], meas.rearrange("(p t) s -> p t s", t=PACK)[:, t, :])
+            meas_sb.append(m_t)
+        w3_raw = tile([P, PACK, N], F32, "w3_raw")
+        nc.sync.dma_start(w3_raw[:], w3.rearrange("(p j) c -> p j c", j=PACK))
+        brn_sb = sb.tile([P, S // 16], U16, name="brn_sb")
+        nc.sync.dma_start(brn_sb[:], brn)
+        unit_sb = tile([P, PACK], F32, "unit_sb")
+        nc.sync.dma_start(unit_sb[:], unit.rearrange("(p t) o -> p (t o)", t=PACK))
+
+        ident = tile([P, P], F32, "ident")
+        make_identity(nc, ident[:])
+        ones = tile([P, 1], F32, "ones")
+        nc.gpsimd.memset(ones[:], 1.0)
+        clutter = tile([P, 1], F32, "clutter")
+        nc.gpsimd.tensor_scalar(clutter[:], ones[:], 0.3, None, ALU.mult)
+
+        x_sc = tile([P, S], U8, "x_sc")
+        nc.vector.tensor_copy(x_sc[:], xs_table[:].indirect(offs_sb[:]))
+        x_q = tile([P, S], U32, "x_q")
+        nc.vector.tensor_copy(x_q[:], xw_table[:].indirect(offs_sb[:]))
+
+        def first_layer(raw_halves, name):
+            grouped = tile([P, PACK, P, PACK], BF16, name + "_bf")
+            for h in range(2):
+                nc.vector.tensor_copy(
+                    grouped[:, :, h * (P // 2) : (h + 1) * (P // 2), :].rearrange("p t m j -> p m j t"),
+                    raw_halves[h][:].rearrange("p j (m t) -> p m j t", t=PACK),
+                )
+            banks = []
+            for t in range(PACK):
+                codes = tile([P, P], U32, "%s_q%d" % (name, t))
+                scales = tile([P, P], U8, "%s_s%d" % (name, t))
+                nc.vector.quantize_mx(codes[:].bitcast(FP8X4), scales[:], grouped[:, t].rearrange("p m j -> p (m j)"))
+                acc = bank("%s_acc%d" % (name, t), "%s_bank%d" % (name, t))
+                nc.tensor.matmul_mx(
+                    acc[:], lhsT=codes[:].bitcast(FP8X4), lhsT_scale=scales[:],
+                    rhs=x_q[:].bitcast(FP8X4), rhs_scale=x_sc[:], start=True, stop=True,
+                )
+                banks.append(acc)
+            return banks
+
+        wg = first_layer(w2_raw, "w2")
+        sig = tile([P, PACK, S], F32, "sig")
+        for t in range(PACK):
+            nc.scalar.activation(sig[:, t, :], wg[t][:], ACT.Sigmoid, scale=-1.0)
+        lnsig = tile([P, PACK, S], F32, "lnsig")
+        nc.scalar.activation(lnsig[:], sig[:], ACT.Ln, bias=LN_FLOOR)
+
+        mu = first_layer(w1_raw, "w1")
+        diff = []
+        for t in range(PACK):
+            d_t = tile([P, S], F32, "diff%d" % t)
+            nc.vector.tensor_tensor(d_t[:], mu[t][:], meas_sb[t][:], ALU.subtract)
+            diff.append(d_t)
+        wei = []
+        for t in range(PACK):
+            w_t = tile([P, S], F32, "wei%d" % t)
+            nc.vector.scalar_tensor_tensor(w_t[:], lnsig[:, t, :], -1.0, wg[t][:], ALU.mult, ALU.max)
+            wei.append(w_t)
+
+        w3_bf = tile([P, N, PACK], BF16, "w3_bf")
+        nc.vector.tensor_copy(
+            w3_bf[:].rearrange("p (c i) j -> p c j i", i=4), w3_raw[:].rearrange("p j (c i) -> p c j i", i=4)
+        )
+        w3_q = tile([P, N], U32, "w3_q")
+        w3_s = tile([P, N], U8, "w3_s")
+        nc.vector.quantize_mx(w3_q[:].bitcast(FP8X4), w3_s[:], w3_bf[:].rearrange("p c j -> p (c j)"))
+        unit5 = tile([P, PACK], F32, "unit5")
+        nc.vector.tensor_scalar(unit5[:], unit_sb[:], 0.2, None, ALU.mult)
+
+        lik = []
+        for t in range(PACK):
+            nc.scalar.activation(sig[:, t, :], diff[t][:], ACT.Tanh)
+            nc.scalar.activation(diff[t][:], sig[:, t, :], ACT.Square)
+            l_t = tile([P, S], F32, "lik%d" % t)
+            nc.scalar.activation(l_t[:], diff[t][:], ACT.Exp, scale=-1.5)
+            lik.append(l_t)
+
+        num, den_t = [], []
+        for t in range(PACK):
+            n_t = tile([P, S], F32, "num%d" % t)
+            nc.vector.tensor_tensor(n_t[:], wei[t][:], lik[t][:], ALU.mult)
+            num.append(n_t)
+            acc = bank("den_t%d" % t, "w2_bank%d" % t)
+            members = n_t[:].rearrange("p (v d) -> p v d", d=D)
+            nc.tensor.matmul(
+                acc[:, :P], lhsT=clutter[:].to_broadcast([P, GROUPS]), rhs=ident[:],
+                is_transpose=True, start=True, stop=False,
+            )
+            for d in range(D):
+                nc.tensor.matmul(
+                    acc[:, :P], lhsT=members[:, :, d], rhs=ident[:], is_transpose=True, start=False, stop=(d == D - 1)
+                )
+            den_t.append(acc)
+
+        upd4, ub = [], []
+        for t in range(PACK):
+            rden_t = tile([P, P], F32, "rden_t%d" % t)
+            nc.vector.reciprocal(rden_t[:], den_t[t][:, :P])
+            rden = bank("rden%d" % t, "w2_bank%d" % t)
+            nc.tensor.transpose(rden[:, :GROUPS], rden_t[:], ident[:])
+            u_t = tile([P, S], F32, "upd4_%d" % t)
+            nc.vector.scalar_tensor_tensor(
+                u_t[:].rearrange("p (v d) -> p v d", d=D),
+                num[t][:].rearrange("p (v d) -> p v d", d=D),
+                4.0,
+                rden[:, :GROUPS].unsqueeze(2).to_broadcast([P, GROUPS, D]),
+                ALU.mult, ALU.mult,
+            )
+            upd4.append(u_t)
+            ub_t = tile([P, S], F32, "ub%d" % t)
+            for h in range(2):
+                nc.scalar.activation(
+                    ub_t[:, h * HALF : (h + 1) * HALF],
+                    u_t[:].indirect(brn_sb[:, h * (HALF // 16) : (h + 1) * (HALF // 16)]),
+                    ACT.Copy,
+                )
+            ub.append(ub_t)
+
+        mix = []
+        for t in range(PACK):
+            m_t = tile([P, S], F32, "mix%d" % t)
+            nc.vector.tensor_tensor(m_t[:], wei[t][:], upd4[t][:], ALU.add)
+            mix.append(m_t)
+
+        out_view = out.rearrange("(b p) s -> p b s", p=P)
+
+        def last_layer(piece, hid, first, lo, width, interleave):
+            hid_il = tile([P, width, PACK], BF16, "hid_il%d" % piece)
+            interleave(
+                hid_il[:].rearrange("p (c i) t -> p c t i", i=4),
+                hid[:, :, lo : lo + width].rearrange("p t (c i) -> p c t i", i=4),
+            )
+            hid_q = tile([P, width], U32, "hid_q%d" % piece)
+            hid_s = tile([P, width], U8, "hid_s%d" % piece)
+            nc.vector.quantize_mx(hid_q[:].bitcast(FP8X4), hid_s[:], hid_il[:].rearrange("p c t -> p (c t)"))
+            acc = bank("out_acc%d" % piece, "w2_bank%d" % piece)
+            for b in range(N // P):
+                nc.tensor.matmul_mx(
+                    acc[:, b * width : (b + 1) * width],
+                    lhsT=w3_q[:, b * P : (b + 1) * P].bitcast(FP8X4), lhsT_scale=w3_s[:, b * P : (b + 1) * P],
+                    rhs=hid_q[:].bitcast(FP8X4), rhs_scale=hid_s[:], start=True, stop=True,
+                )
+            res = tile([P, N // P, width], F32, "res%d" % piece)
+            nc.scalar.copy(res[:].rearrange("p b s -> p (b s)"), acc[:, : (N // P) * width])
+            nc.sync.dma_start(out_view[:, :, first + lo : first + lo + width], res[:])
+
+        for h in range(2):
+            cols = slice(h * HALF, (h + 1) * HALF)
+            hid = tile([P, PACK, HALF], BF16, "hid%d" % h)
+            spawn = []
+            for t in range(PACK):
+                g_t = tile([P, HALF], F32, "g%d_%d" % (h, t))
+                nc.vector.scalar_tensor_tensor(g_t[:], ub[t][:, cols], 0.7 / 4.0, mu[t][:, cols], ALU.mult, ALU.add)
+                spawn.append(g_t)
+            for t in range(PACK):
+                nc.vector.scalar_tensor_tensor(
+                    hid[:, t, :], mix[t][:, cols], unit5[:, t : t + 1], spawn[t][:], ALU.mult, ALU.mult
+                )
+            if h == 0:
+                last_layer(0, hid, 0, 0, HALF, nc.scalar.copy)
+            else:
+                last_layer(1, hid, HALF, 0, HALF // 2, nc.vector.tensor_copy)
+                last_layer(2, hid, HALF, HALF // 2, HALF // 2, nc.scalar.copy)

@@ -29,8 +29,8 @@ def tile_picked_ygmphd_mean_p_kernel(tc, x_words, x_scales, w1, w2, meas, unit, 
         sb = ctx.enter_context(tc.tile_pool(name="sb", bufs=1))
         ps = ctx.enter_context(tc.psum_pool(name="ps", bufs=1))
 
-        def tile(shape, dtype, name):
-            return sb.tile(shape, dtype, name=name, align_bytes=64)
+        def tile(shape, dtype, name, tag=None):
+            return sb.tile(shape, dtype, name=name, tag=tag or name, align_bytes=64)
 
         def bank(name, tag):
             return ps.tile([P, S], F32, name=name, tag=tag)
@@ -80,10 +80,10 @@ def tile_picked_ygmphd_mean_p_kernel(tc, x_words, x_scales, w1, w2, meas, unit, 
         x_q = tile([P, S], U32, "x_q")
         nc.vector.tensor_copy(x_q[:], xw_table[:].indirect(offs_sb[:]))
 
-        def first_layer(raw_halves, name):
-            grouped = tile([P, PACK, P, PACK], BF16, name + "_bf")
+        def first_layer(raw_halves, name, casts):
+            grouped = tile([P, PACK, P, PACK], BF16, name + "_bf", "w_bf")
             for h in range(2):
-                nc.vector.tensor_copy(
+                casts[h](
                     grouped[:, :, h * (P // 2) : (h + 1) * (P // 2), :].rearrange("p t m j -> p m j t"),
                     raw_halves[h][:].rearrange("p j (m t) -> p m j t", t=PACK),
                 )
@@ -100,14 +100,14 @@ def tile_picked_ygmphd_mean_p_kernel(tc, x_words, x_scales, w1, w2, meas, unit, 
                 banks.append(acc)
             return banks
 
-        wg = first_layer(w2_raw, "w2")
+        wg = first_layer(w2_raw, "w2", (nc.scalar.copy, nc.vector.tensor_copy))
         sig = tile([P, PACK, S], F32, "sig")
         for t in range(PACK):
             nc.scalar.activation(sig[:, t, :], wg[t][:], ACT.Sigmoid, scale=-1.0)
         lnsig = tile([P, PACK, S], F32, "lnsig")
         nc.scalar.activation(lnsig[:], sig[:], ACT.Ln, bias=LN_FLOOR)
 
-        mu = first_layer(w1_raw, "w1")
+        mu = first_layer(w1_raw, "w1", (nc.vector.tensor_copy, nc.vector.tensor_copy))
         diff = []
         for t in range(PACK):
             d_t = tile([P, S], F32, "diff%d" % t)
@@ -131,62 +131,66 @@ def tile_picked_ygmphd_mean_p_kernel(tc, x_words, x_scales, w1, w2, meas, unit, 
 
         lik = []
         for t in range(PACK):
-            nc.scalar.activation(sig[:, t, :], diff[t][:], ACT.Tanh)
-            nc.scalar.activation(diff[t][:], sig[:, t, :], ACT.Square)
+            th = sig[:, t % 2, :]
+            nc.scalar.activation(th, diff[t][:], ACT.Tanh)
+            sq = tile([P, S], F32, "sq%d" % t, "sq%d" % (t // 2))
+            if t == 0:
+                nc.vector.tensor_tensor(sq[:], th, th, ALU.mult)
+            else:
+                nc.scalar.activation(sq[:], th, ACT.Square)
             l_t = tile([P, S], F32, "lik%d" % t)
-            nc.scalar.activation(l_t[:], diff[t][:], ACT.Exp, scale=-1.5)
+            nc.scalar.activation(l_t[:], sq[:], ACT.Exp, scale=-1.5)
             lik.append(l_t)
 
-        num, den_t = [], []
+        mix, ub = [], []
         for t in range(PACK):
-            n_t = tile([P, S], F32, "num%d" % t)
-            nc.vector.tensor_tensor(n_t[:], wei[t][:], lik[t][:], ALU.mult)
-            num.append(n_t)
-            acc = bank("den_t%d" % t, "w2_bank%d" % t)
-            members = n_t[:].rearrange("p (v d) -> p v d", d=D)
-            nc.tensor.matmul(
-                acc[:, :P], lhsT=clutter[:].to_broadcast([P, GROUPS]), rhs=ident[:],
-                is_transpose=True, start=True, stop=False,
-            )
-            for d in range(D):
+            num = tile([P, S], F32, "num%d" % t, "num%d" % (0 if t == 2 else t))
+            nc.vector.tensor_tensor(num[:], wei[t][:], lik[t][:], ALU.mult)
+            members = num[:].rearrange("p (v d) -> p v d", d=D)
+            if t == 0:
+                pairs = tile([P, GROUPS, 2], F32, "pairs")
+                nc.vector.tensor_tensor(pairs[:], members[:, :, 0:2], members[:, :, 2:4], ALU.add)
+                den = tile([P, GROUPS], F32, "den")
+                nc.vector.scalar_tensor_tensor(den[:], pairs[:, :, 0], 0.3, pairs[:, :, 1], ALU.add, ALU.add)
+                rden = tile([P, GROUPS], F32, "rden0")
+                nc.vector.reciprocal(rden[:], den[:])
+            else:
+                den_t = bank("den_t%d" % t, "w2_bank%d" % t)
                 nc.tensor.matmul(
-                    acc[:, :P], lhsT=members[:, :, d], rhs=ident[:], is_transpose=True, start=False, stop=(d == D - 1)
+                    den_t[:, :P], lhsT=clutter[:].to_broadcast([P, GROUPS]), rhs=ident[:],
+                    is_transpose=True, start=True, stop=False,
                 )
-            den_t.append(acc)
-
-        upd4, ub = [], []
-        for t in range(PACK):
-            rden_t = tile([P, P], F32, "rden_t%d" % t)
-            nc.vector.reciprocal(rden_t[:], den_t[t][:, :P])
-            rden = bank("rden%d" % t, "w2_bank%d" % t)
-            nc.tensor.transpose(rden[:, :GROUPS], rden_t[:], ident[:])
-            u_t = tile([P, S], F32, "upd4_%d" % t)
+                for d in range(D):
+                    nc.tensor.matmul(
+                        den_t[:, :P], lhsT=members[:, :, d], rhs=ident[:],
+                        is_transpose=True, start=False, stop=(d == D - 1),
+                    )
+                rden_t = tile([P, P], F32, "rden_t%d" % t)
+                nc.vector.reciprocal(rden_t[:], den_t[:, :P])
+                rden = bank("rden%d" % t, "w2_bank%d" % t)
+                nc.tensor.transpose(rden[:, :GROUPS], rden_t[:], ident[:])
+            upd4 = tile([P, S], F32, "upd4_%d" % t)
             nc.vector.scalar_tensor_tensor(
-                u_t[:].rearrange("p (v d) -> p v d", d=D),
-                num[t][:].rearrange("p (v d) -> p v d", d=D),
+                upd4[:].rearrange("p (v d) -> p v d", d=D),
+                members,
                 4.0,
                 rden[:, :GROUPS].unsqueeze(2).to_broadcast([P, GROUPS, D]),
                 ALU.mult, ALU.mult,
             )
-            upd4.append(u_t)
             ub_t = tile([P, S], F32, "ub%d" % t)
-            for h in range(2):
-                nc.scalar.activation(
-                    ub_t[:, h * HALF : (h + 1) * HALF],
-                    u_t[:].indirect(brn_sb[:, h * (HALF // 16) : (h + 1) * (HALF // 16)]),
-                    ACT.Copy,
-                )
-            ub.append(ub_t)
-
-        mix = []
-        for t in range(PACK):
             m_t = tile([P, S], F32, "mix%d" % t)
-            nc.vector.tensor_tensor(m_t[:], wei[t][:], upd4[t][:], ALU.add)
+            for h in range(2):
+                cols = slice(h * HALF, (h + 1) * HALF)
+                nc.scalar.activation(
+                    ub_t[:, cols], upd4[:].indirect(brn_sb[:, h * (HALF // 16) : (h + 1) * (HALF // 16)]), ACT.Copy
+                )
+                nc.gpsimd.tensor_tensor(m_t[:, cols], wei[t][:, cols], upd4[:, cols], ALU.add)
+            ub.append(ub_t)
             mix.append(m_t)
 
         out_view = out.rearrange("(b p) s -> p b s", p=P)
 
-        def last_layer(piece, hid, first, lo, width, interleave):
+        def last_layer(piece, hid, first, lo, width, interleave, evacuate):
             hid_il = tile([P, width, PACK], BF16, "hid_il%d" % piece)
             interleave(
                 hid_il[:].rearrange("p (c i) t -> p c t i", i=4),
@@ -203,7 +207,7 @@ def tile_picked_ygmphd_mean_p_kernel(tc, x_words, x_scales, w1, w2, meas, unit, 
                     rhs=hid_q[:].bitcast(FP8X4), rhs_scale=hid_s[:], start=True, stop=True,
                 )
             res = tile([P, N // P, width], F32, "res%d" % piece)
-            nc.scalar.copy(res[:].rearrange("p b s -> p (b s)"), acc[:, : (N // P) * width])
+            evacuate(res[:].rearrange("p b s -> p (b s)"), acc[:, : (N // P) * width])
             nc.sync.dma_start(out_view[:, :, first + lo : first + lo + width], res[:])
 
         for h in range(2):
@@ -219,7 +223,7 @@ def tile_picked_ygmphd_mean_p_kernel(tc, x_words, x_scales, w1, w2, meas, unit, 
                     hid[:, t, :], mix[t][:, cols], unit5[:, t : t + 1], spawn[t][:], ALU.mult, ALU.mult
                 )
             if h == 0:
-                last_layer(0, hid, 0, 0, HALF, nc.scalar.copy)
+                last_layer(0, hid, 0, 0, HALF, nc.scalar.copy, nc.scalar.copy)
             else:
-                last_layer(1, hid, HALF, 0, HALF // 2, nc.vector.tensor_copy)
-                last_layer(2, hid, HALF, HALF // 2, HALF // 2, nc.scalar.copy)
+                last_layer(1, hid, HALF, 0, HALF // 2, nc.vector.tensor_copy, nc.scalar.copy)
+                last_layer(2, hid, HALF, HALF // 2, HALF // 2, nc.scalar.copy, nc.vector.tensor_copy)

@@ -39,12 +39,12 @@ def tile_picked_ygmphd_mean_p_kernel(tc, x_words, x_scales, w1, w2, meas, unit, 
         nc.sync.dma_start(offs_sb[:], offs)
         xs_table = tile([P, T], U8, "xs_table")
         nc.vector.memset(xs_table[:].bitcast(I32), 0)
-        xw_table = tile([P, T], U32, "xw_table")
-        nc.sync.dma_start(xw_table[:].bitcast(I32), x_words[0].rearrange("p n r -> p (n r)").bitcast(I32))
         for q in range(4):
             nc.sync.dma_start(
                 xs_table[32 * q : 32 * q + 4, :].bitcast(I32), x_scales[0, 4 * q : 4 * q + 4, :].bitcast(I32)
             )
+        xw_table = tile([P, T], U32, "xw_table")
+        nc.sync.dma_start(xw_table[:].bitcast(I32), x_words[0].rearrange("p n r -> p (n r)").bitcast(I32))
 
         def load_halves(w, name):
             halves = []
@@ -142,7 +142,7 @@ def tile_picked_ygmphd_mean_p_kernel(tc, x_words, x_scales, w1, w2, meas, unit, 
             nc.scalar.activation(l_t[:], sq[:], ACT.Exp, scale=-1.5)
             lik.append(l_t)
 
-        mix, ub = [], []
+        mix, ub, upd = [], [], []
         for t in range(PACK):
             num = tile([P, S], F32, "num%d" % t, "num%d" % (0 if t == 2 else t))
             nc.vector.tensor_tensor(num[:], wei[t][:], lik[t][:], ALU.mult)
@@ -178,23 +178,33 @@ def tile_picked_ygmphd_mean_p_kernel(tc, x_words, x_scales, w1, w2, meas, unit, 
                 ALU.mult, ALU.mult,
             )
             ub_t = tile([P, S], F32, "ub%d" % t)
-            m_t = tile([P, S], F32, "mix%d" % t)
             for h in range(2):
                 cols = slice(h * HALF, (h + 1) * HALF)
                 nc.scalar.activation(
                     ub_t[:, cols], upd4[:].indirect(brn_sb[:, h * (HALF // 16) : (h + 1) * (HALF // 16)]), ACT.Copy
                 )
-                nc.gpsimd.tensor_tensor(m_t[:, cols], wei[t][:, cols], upd4[:, cols], ALU.add)
             ub.append(ub_t)
+            upd.append(upd4)
+
+        for t in range(PACK):
+            m_t = tile([P, S], F32, "mix%d" % t, "lik%d" % (PACK - 1 - t))
+            for h in range(2):
+                cols = slice(h * HALF, (h + 1) * HALF)
+                nc.gpsimd.tensor_tensor(m_t[:, cols], wei[t][:, cols], upd[t][:, cols], ALU.add)
             mix.append(m_t)
+        spawn = []
+        for t in range(PACK):
+            g_t = tile([P, S], F32, "g%d" % t)
+            nc.vector.scalar_tensor_tensor(g_t[:], ub[t][:], 0.7 / 4.0, mu[t][:], ALU.mult, ALU.add)
+            spawn.append(g_t)
 
         out_view = out.rearrange("(b p) s -> p b s", p=P)
 
-        def last_layer(piece, hid, first, lo, width, interleave, evacuate):
+        def last_layer(piece, hid, first, lo, width, interleave, evacuate, queue):
             hid_il = tile([P, width, PACK], BF16, "hid_il%d" % piece)
             interleave(
                 hid_il[:].rearrange("p (c i) t -> p c t i", i=4),
-                hid[:, :, lo : lo + width].rearrange("p t (c i) -> p c t i", i=4),
+                hid[:, :, first + lo : first + lo + width].rearrange("p t (c i) -> p c t i", i=4),
             )
             hid_q = tile([P, width], U32, "hid_q%d" % piece)
             hid_s = tile([P, width], U8, "hid_s%d" % piece)
@@ -208,22 +218,17 @@ def tile_picked_ygmphd_mean_p_kernel(tc, x_words, x_scales, w1, w2, meas, unit, 
                 )
             res = tile([P, N // P, width], F32, "res%d" % piece)
             evacuate(res[:].rearrange("p b s -> p (b s)"), acc[:, : (N // P) * width])
-            nc.sync.dma_start(out_view[:, :, first + lo : first + lo + width], res[:])
+            queue.dma_start(out_view[:, :, first + lo : first + lo + width], res[:])
 
+        hid = tile([P, PACK, S], BF16, "hid", "num3")
         for h in range(2):
             cols = slice(h * HALF, (h + 1) * HALF)
-            hid = tile([P, PACK, HALF], BF16, "hid%d" % h)
-            spawn = []
-            for t in range(PACK):
-                g_t = tile([P, HALF], F32, "g%d_%d" % (h, t))
-                nc.vector.scalar_tensor_tensor(g_t[:], ub[t][:, cols], 0.7 / 4.0, mu[t][:, cols], ALU.mult, ALU.add)
-                spawn.append(g_t)
             for t in range(PACK):
                 nc.vector.scalar_tensor_tensor(
-                    hid[:, t, :], mix[t][:, cols], unit5[:, t : t + 1], spawn[t][:], ALU.mult, ALU.mult
+                    hid[:, t, cols], mix[t][:, cols], unit5[:, t : t + 1], spawn[t][:, cols], ALU.mult, ALU.mult
                 )
             if h == 0:
-                last_layer(0, hid, 0, 0, HALF, nc.scalar.copy, nc.scalar.copy)
+                last_layer(0, hid, 0, 0, HALF, nc.scalar.copy, nc.scalar.copy, nc.sync)
             else:
-                last_layer(1, hid, HALF, 0, HALF // 2, nc.vector.tensor_copy, nc.scalar.copy)
-                last_layer(2, hid, HALF, HALF // 2, HALF // 2, nc.scalar.copy, nc.vector.tensor_copy)
+                last_layer(1, hid, HALF, 0, HALF // 2, nc.vector.tensor_copy, nc.scalar.copy, nc.sync)
+                last_layer(2, hid, HALF, HALF // 2, HALF // 2, nc.scalar.copy, nc.vector.tensor_copy, nc.sync)

@@ -133,8 +133,8 @@ def tile_picked_ygmphd_mean_p_kernel(tc, x_words, x_scales, w1, w2, meas, unit, 
         for t in range(PACK):
             th = sig[:, t % 2, :]
             nc.scalar.activation(th, diff[t][:], ACT.Tanh)
-            sq = tile([P, S], F32, "sq%d" % t, "sq%d" % (t // 2))
-            if t == 0:
+            sq = tile([P, S], F32, "sq%d" % t)
+            if t < 2:
                 nc.vector.tensor_tensor(sq[:], th, th, ALU.mult)
             else:
                 nc.scalar.activation(sq[:], th, ACT.Square)
@@ -145,7 +145,12 @@ def tile_picked_ygmphd_mean_p_kernel(tc, x_words, x_scales, w1, w2, meas, unit, 
         mix, ub, upd = [], [], []
         for t in range(PACK):
             num = tile([P, S], F32, "num%d" % t, "num%d" % (0 if t == 2 else t))
-            nc.vector.tensor_tensor(num[:], wei[t][:], lik[t][:], ALU.mult)
+            if t == PACK - 1:
+                for h in range(2):
+                    cols = slice(h * HALF, (h + 1) * HALF)
+                    nc.gpsimd.tensor_tensor(num[:, cols], wei[t][:, cols], lik[t][:, cols], ALU.mult)
+            else:
+                nc.vector.tensor_tensor(num[:], wei[t][:], lik[t][:], ALU.mult)
             members = num[:].rearrange("p (v d) -> p v d", d=D)
             if t == 0:
                 pairs = tile([P, GROUPS, 2], F32, "pairs")
@@ -228,7 +233,8 @@ def tile_picked_ygmphd_mean_p_kernel(tc, x_words, x_scales, w1, w2, meas, unit, 
                     hid[:, t, cols], mix[t][:, cols], unit5[:, t : t + 1], spawn[t][:, cols], ALU.mult, ALU.mult
                 )
             if h == 0:
-                last_layer(0, hid, 0, 0, HALF, nc.scalar.copy, nc.scalar.copy, nc.sync)
+                last_layer(0, hid, 0, 0, HALF // 2, nc.scalar.copy, nc.scalar.copy, nc.sync)
+                last_layer(1, hid, 0, HALF // 2, HALF // 2, nc.scalar.copy, nc.scalar.copy, nc.sync)
             else:
-                last_layer(1, hid, HALF, 0, HALF // 2, nc.vector.tensor_copy, nc.scalar.copy, nc.sync)
-                last_layer(2, hid, HALF, HALF // 2, HALF // 2, nc.scalar.copy, nc.vector.tensor_copy, nc.sync)
+                last_layer(2, hid, HALF, 0, HALF // 2, nc.vector.tensor_copy, nc.scalar.copy, nc.sync)
+                last_layer(3, hid, HALF, HALF // 2, HALF // 2, nc.scalar.copy, nc.vector.tensor_copy, nc.sync)

@@ -18,13 +18,23 @@ ACT = mybir.ActivationFunctionType
 
 P = 128
 PACK = 4
+LIST_ROWS = 16
+SCALE_ROWS = 4
 HALF = S // 2
+PIECE = S // 4
 GROUPS = S // D
+LAST = PACK - 1
 LN_FLOOR = 2.0**-60
+CLUTTER = 0.3
+UPD_SCALE = 0.8 / 0.2
+VECTOR_SQUARES = 2
 
 
-def tile_picked_ygmphd_mean_p_kernel(tc, x_words, x_scales, w1, w2, meas, unit, w3, offs, brn, out):
+def tile_picked_ygmphd_mean_p_kernel(
+    tc, x_words, x_scales, w1, w2, meas, unit, w3, offs, brn, out
+):
     nc = tc.nc
+    halves = [slice(h * HALF, (h + 1) * HALF) for h in range(2)]
     with ExitStack() as ctx:
         sb = ctx.enter_context(tc.tile_pool(name="sb", bufs=1))
         ps = ctx.enter_context(tc.psum_pool(name="ps", bufs=1))
@@ -35,35 +45,37 @@ def tile_picked_ygmphd_mean_p_kernel(tc, x_words, x_scales, w1, w2, meas, unit, 
         def bank(name, tag):
             return ps.tile([P, S], F32, name=name, tag=tag)
 
-        offs_sb = sb.tile([P, S // 16], U16, name="offs_sb")
+        offs_sb = sb.tile([P, S // LIST_ROWS], U16, name="offs_sb")
         nc.sync.dma_start(offs_sb[:], offs)
         xs_table = tile([P, T], U8, "xs_table")
         nc.vector.memset(xs_table[:].bitcast(I32), 0)
-        for q in range(4):
+        for q in range(P // 32):
             nc.sync.dma_start(
-                xs_table[32 * q : 32 * q + 4, :].bitcast(I32), x_scales[0, 4 * q : 4 * q + 4, :].bitcast(I32)
+                xs_table[32 * q : 32 * q + SCALE_ROWS, :].bitcast(I32),
+                x_scales[0, SCALE_ROWS * q : SCALE_ROWS * (q + 1), :].bitcast(I32),
             )
         xw_table = tile([P, T], U32, "xw_table")
         nc.sync.dma_start(xw_table[:].bitcast(I32), x_words[0].rearrange("p n r -> p (n r)").bitcast(I32))
 
         def load_halves(w, name):
-            halves = []
+            rows = w.rearrange("(p j) c -> p j c", j=PACK)
+            raws = []
             for h in range(2):
                 raw = tile([P, PACK, H // 2], F32, "%s_raw%d" % (name, h))
-                nc.sync.dma_start(raw[:], w.rearrange("(p j) c -> p j c", j=PACK)[:, :, h * (H // 2) : (h + 1) * (H // 2)])
-                halves.append(raw)
-            return halves
+                nc.sync.dma_start(raw[:], rows[:, :, h * (H // 2) : (h + 1) * (H // 2)])
+                raws.append(raw)
+            return raws
 
         w2_raw = load_halves(w2, "w2")
         w1_raw = load_halves(w1, "w1")
         meas_sb = []
         for t in range(PACK):
-            m_t = tile([P, S], F32, "meas%d" % t)
-            nc.sync.dma_start(m_t[:], meas.rearrange("(p t) s -> p t s", t=PACK)[:, t, :])
-            meas_sb.append(m_t)
+            meas_t = tile([P, S], F32, "meas%d" % t)
+            nc.sync.dma_start(meas_t[:], meas.rearrange("(p t) s -> p t s", t=PACK)[:, t, :])
+            meas_sb.append(meas_t)
         w3_raw = tile([P, PACK, N], F32, "w3_raw")
         nc.sync.dma_start(w3_raw[:], w3.rearrange("(p j) c -> p j c", j=PACK))
-        brn_sb = sb.tile([P, S // 16], U16, name="brn_sb")
+        brn_sb = sb.tile([P, S // LIST_ROWS], U16, name="brn_sb")
         nc.sync.dma_start(brn_sb[:], brn)
         unit_sb = tile([P, PACK], F32, "unit_sb")
         nc.sync.dma_start(unit_sb[:], unit.rearrange("(p t) o -> p (t o)", t=PACK))
@@ -73,32 +85,35 @@ def tile_picked_ygmphd_mean_p_kernel(tc, x_words, x_scales, w1, w2, meas, unit, 
         ones = tile([P, 1], F32, "ones")
         nc.gpsimd.memset(ones[:], 1.0)
         clutter = tile([P, 1], F32, "clutter")
-        nc.gpsimd.tensor_scalar(clutter[:], ones[:], 0.3, None, ALU.mult)
+        nc.gpsimd.tensor_scalar(clutter[:], ones[:], CLUTTER, None, ALU.mult)
+
+        warm = tile([P, 1], F32, "warm")
+        nc.scalar.activation(warm[:], ones[:], ACT.Sigmoid)
 
         x_sc = tile([P, S], U8, "x_sc")
         nc.vector.tensor_copy(x_sc[:], xs_table[:].indirect(offs_sb[:]))
         x_q = tile([P, S], U32, "x_q")
         nc.vector.tensor_copy(x_q[:], xw_table[:].indirect(offs_sb[:]))
 
-        def first_layer(raw_halves, name, casts):
-            grouped = tile([P, PACK, P, PACK], BF16, name + "_bf", "w_bf")
+        def first_layer(raws, name, casts):
+            dealt = tile([P, PACK, P, PACK], BF16, name + "_bf", "w_bf")
             for h in range(2):
                 casts[h](
-                    grouped[:, :, h * (P // 2) : (h + 1) * (P // 2), :].rearrange("p t m j -> p m j t"),
-                    raw_halves[h][:].rearrange("p j (m t) -> p m j t", t=PACK),
+                    dealt[:, :, h * (P // 2) : (h + 1) * (P // 2), :].rearrange("p t m j -> p m j t"),
+                    raws[h][:].rearrange("p j (m t) -> p m j t", t=PACK),
                 )
-            banks = []
+            planes = []
             for t in range(PACK):
                 codes = tile([P, P], U32, "%s_q%d" % (name, t))
                 scales = tile([P, P], U8, "%s_s%d" % (name, t))
-                nc.vector.quantize_mx(codes[:].bitcast(FP8X4), scales[:], grouped[:, t].rearrange("p m j -> p (m j)"))
+                nc.vector.quantize_mx(codes[:].bitcast(FP8X4), scales[:], dealt[:, t].rearrange("p m j -> p (m j)"))
                 acc = bank("%s_acc%d" % (name, t), "%s_bank%d" % (name, t))
                 nc.tensor.matmul_mx(
                     acc[:], lhsT=codes[:].bitcast(FP8X4), lhsT_scale=scales[:],
                     rhs=x_q[:].bitcast(FP8X4), rhs_scale=x_sc[:], start=True, stop=True,
                 )
-                banks.append(acc)
-            return banks
+                planes.append(acc)
+            return planes
 
         wg = first_layer(w2_raw, "w2", (nc.scalar.copy, nc.vector.tensor_copy))
         sig = tile([P, PACK, S], F32, "sig")
@@ -110,14 +125,14 @@ def tile_picked_ygmphd_mean_p_kernel(tc, x_words, x_scales, w1, w2, meas, unit, 
         mu = first_layer(w1_raw, "w1", (nc.vector.tensor_copy, nc.vector.tensor_copy))
         diff = []
         for t in range(PACK):
-            d_t = tile([P, S], F32, "diff%d" % t)
-            nc.vector.tensor_tensor(d_t[:], mu[t][:], meas_sb[t][:], ALU.subtract)
-            diff.append(d_t)
+            diff_t = tile([P, S], F32, "diff%d" % t)
+            nc.vector.tensor_tensor(diff_t[:], mu[t][:], meas_sb[t][:], ALU.subtract)
+            diff.append(diff_t)
         wei = []
         for t in range(PACK):
-            w_t = tile([P, S], F32, "wei%d" % t)
-            nc.vector.scalar_tensor_tensor(w_t[:], lnsig[:, t, :], -1.0, wg[t][:], ALU.mult, ALU.max)
-            wei.append(w_t)
+            wei_t = tile([P, S], F32, "wei%d" % t)
+            nc.vector.scalar_tensor_tensor(wei_t[:], lnsig[:, t, :], -1.0, wg[t][:], ALU.mult, ALU.max)
+            wei.append(wei_t)
 
         w3_bf = tile([P, N, PACK], BF16, "w3_bf")
         nc.vector.tensor_copy(
@@ -126,28 +141,27 @@ def tile_picked_ygmphd_mean_p_kernel(tc, x_words, x_scales, w1, w2, meas, unit, 
         w3_q = tile([P, N], U32, "w3_q")
         w3_s = tile([P, N], U8, "w3_s")
         nc.vector.quantize_mx(w3_q[:].bitcast(FP8X4), w3_s[:], w3_bf[:].rearrange("p c j -> p (c j)"))
-        unit5 = tile([P, PACK], F32, "unit5")
-        nc.vector.tensor_scalar(unit5[:], unit_sb[:], 0.2, None, ALU.mult)
+        row_factor = tile([P, PACK], F32, "row_factor")
+        nc.vector.tensor_scalar(row_factor[:], unit_sb[:], 0.2, None, ALU.mult)
 
         lik = []
         for t in range(PACK):
-            th = sig[:, t % 2, :]
-            nc.scalar.activation(th, diff[t][:], ACT.Tanh)
-            sq = tile([P, S], F32, "sq%d" % t)
-            if t < 2:
-                nc.vector.tensor_tensor(sq[:], th, th, ALU.mult)
+            tanh_t = sig[:, t % 2, :]
+            nc.scalar.activation(tanh_t, diff[t][:], ACT.Tanh)
+            square = tile([P, S], F32, "square%d" % t)
+            if t < VECTOR_SQUARES:
+                nc.vector.tensor_tensor(square[:], tanh_t, tanh_t, ALU.mult)
             else:
-                nc.scalar.activation(sq[:], th, ACT.Square)
-            l_t = tile([P, S], F32, "lik%d" % t)
-            nc.scalar.activation(l_t[:], sq[:], ACT.Exp, scale=-1.5)
-            lik.append(l_t)
+                nc.scalar.activation(square[:], tanh_t, ACT.Square)
+            lik_t = tile([P, S], F32, "lik%d" % t)
+            nc.scalar.activation(lik_t[:], square[:], ACT.Exp, scale=-1.5)
+            lik.append(lik_t)
 
-        mix, ub, upd = [], [], []
+        upd, picked = [], []
         for t in range(PACK):
             num = tile([P, S], F32, "num%d" % t, "num%d" % (0 if t == 2 else t))
-            if t == PACK - 1:
-                for h in range(2):
-                    cols = slice(h * HALF, (h + 1) * HALF)
+            if t == LAST:
+                for cols in halves:
                     nc.gpsimd.tensor_tensor(num[:, cols], wei[t][:, cols], lik[t][:, cols], ALU.mult)
             else:
                 nc.vector.tensor_tensor(num[:], wei[t][:], lik[t][:], ALU.mult)
@@ -156,85 +170,83 @@ def tile_picked_ygmphd_mean_p_kernel(tc, x_words, x_scales, w1, w2, meas, unit, 
                 pairs = tile([P, GROUPS, 2], F32, "pairs")
                 nc.vector.tensor_tensor(pairs[:], members[:, :, 0:2], members[:, :, 2:4], ALU.add)
                 den = tile([P, GROUPS], F32, "den")
-                nc.vector.scalar_tensor_tensor(den[:], pairs[:, :, 0], 0.3, pairs[:, :, 1], ALU.add, ALU.add)
+                nc.vector.scalar_tensor_tensor(den[:], pairs[:, :, 0], CLUTTER, pairs[:, :, 1], ALU.add, ALU.add)
                 rden = tile([P, GROUPS], F32, "rden0")
                 nc.vector.reciprocal(rden[:], den[:])
             else:
-                den_t = bank("den_t%d" % t, "w2_bank%d" % t)
+                den_turned = bank("den_turned%d" % t, "w2_bank%d" % t)
                 nc.tensor.matmul(
-                    den_t[:, :P], lhsT=clutter[:].to_broadcast([P, GROUPS]), rhs=ident[:],
+                    den_turned[:, :P], lhsT=clutter[:].to_broadcast([P, GROUPS]), rhs=ident[:],
                     is_transpose=True, start=True, stop=False,
                 )
                 for d in range(D):
                     nc.tensor.matmul(
-                        den_t[:, :P], lhsT=members[:, :, d], rhs=ident[:],
+                        den_turned[:, :P], lhsT=members[:, :, d], rhs=ident[:],
                         is_transpose=True, start=False, stop=(d == D - 1),
                     )
-                rden_t = tile([P, P], F32, "rden_t%d" % t)
-                nc.vector.reciprocal(rden_t[:], den_t[:, :P])
+                rden_turned = tile([P, P], F32, "rden_turned%d" % t)
+                nc.vector.reciprocal(rden_turned[:], den_turned[:, :P])
                 rden = bank("rden%d" % t, "w2_bank%d" % t)
-                nc.tensor.transpose(rden[:, :GROUPS], rden_t[:], ident[:])
-            upd4 = tile([P, S], F32, "upd4_%d" % t)
+                nc.tensor.transpose(rden[:, :GROUPS], rden_turned[:], ident[:])
+            upd_t = tile([P, S], F32, "upd%d" % t)
             nc.vector.scalar_tensor_tensor(
-                upd4[:].rearrange("p (v d) -> p v d", d=D),
+                upd_t[:].rearrange("p (v d) -> p v d", d=D),
                 members,
-                4.0,
+                UPD_SCALE,
                 rden[:, :GROUPS].unsqueeze(2).to_broadcast([P, GROUPS, D]),
                 ALU.mult, ALU.mult,
             )
-            ub_t = tile([P, S], F32, "ub%d" % t)
+            picked_t = tile([P, S], F32, "picked%d" % t)
             for h in range(2):
-                cols = slice(h * HALF, (h + 1) * HALF)
-                nc.scalar.activation(
-                    ub_t[:, cols], upd4[:].indirect(brn_sb[:, h * (HALF // 16) : (h + 1) * (HALF // 16)]), ACT.Copy
-                )
-            ub.append(ub_t)
-            upd.append(upd4)
+                offsets = brn_sb[:, h * (HALF // LIST_ROWS) : (h + 1) * (HALF // LIST_ROWS)]
+                nc.scalar.activation(picked_t[:, halves[h]], upd_t[:].indirect(offsets), ACT.Copy)
+            picked.append(picked_t)
+            upd.append(upd_t)
 
+        mix = []
         for t in range(PACK):
-            m_t = tile([P, S], F32, "mix%d" % t, "lik%d" % (PACK - 1 - t))
-            for h in range(2):
-                cols = slice(h * HALF, (h + 1) * HALF)
-                nc.gpsimd.tensor_tensor(m_t[:, cols], wei[t][:, cols], upd[t][:, cols], ALU.add)
-            mix.append(m_t)
+            mix_t = tile([P, S], F32, "mix%d" % t, "lik%d" % (LAST - t))
+            for cols in halves:
+                nc.gpsimd.tensor_tensor(mix_t[:, cols], wei[t][:, cols], upd[t][:, cols], ALU.add)
+            mix.append(mix_t)
         spawn = []
         for t in range(PACK):
-            g_t = tile([P, S], F32, "g%d" % t)
-            nc.vector.scalar_tensor_tensor(g_t[:], ub[t][:], 0.7 / 4.0, mu[t][:], ALU.mult, ALU.add)
-            spawn.append(g_t)
+            spawn_t = tile([P, S], F32, "spawn%d" % t)
+            nc.vector.scalar_tensor_tensor(spawn_t[:], picked[t][:], 0.7 / UPD_SCALE, mu[t][:], ALU.mult, ALU.add)
+            spawn.append(spawn_t)
 
         out_view = out.rearrange("(b p) s -> p b s", p=P)
 
-        def last_layer(piece, hid, first, lo, width, interleave, evacuate, queue):
-            hid_il = tile([P, width, PACK], BF16, "hid_il%d" % piece)
+        def last_layer(piece, hid, interleave, evacuate):
+            cols = slice(piece * PIECE, (piece + 1) * PIECE)
+            packed = tile([P, PIECE, PACK], BF16, "packed%d" % piece)
             interleave(
-                hid_il[:].rearrange("p (c i) t -> p c t i", i=4),
-                hid[:, :, first + lo : first + lo + width].rearrange("p t (c i) -> p c t i", i=4),
+                packed[:].rearrange("p (c i) t -> p c t i", i=4), hid[:, :, cols].rearrange("p t (c i) -> p c t i", i=4)
             )
-            hid_q = tile([P, width], U32, "hid_q%d" % piece)
-            hid_s = tile([P, width], U8, "hid_s%d" % piece)
-            nc.vector.quantize_mx(hid_q[:].bitcast(FP8X4), hid_s[:], hid_il[:].rearrange("p c t -> p (c t)"))
+            hid_q = tile([P, PIECE], U32, "hid_q%d" % piece)
+            hid_s = tile([P, PIECE], U8, "hid_s%d" % piece)
+            nc.vector.quantize_mx(hid_q[:].bitcast(FP8X4), hid_s[:], packed[:].rearrange("p c t -> p (c t)"))
             acc = bank("out_acc%d" % piece, "w2_bank%d" % piece)
             for b in range(N // P):
                 nc.tensor.matmul_mx(
-                    acc[:, b * width : (b + 1) * width],
+                    acc[:, b * PIECE : (b + 1) * PIECE],
                     lhsT=w3_q[:, b * P : (b + 1) * P].bitcast(FP8X4), lhsT_scale=w3_s[:, b * P : (b + 1) * P],
                     rhs=hid_q[:].bitcast(FP8X4), rhs_scale=hid_s[:], start=True, stop=True,
                 )
-            res = tile([P, N // P, width], F32, "res%d" % piece)
-            evacuate(res[:].rearrange("p b s -> p (b s)"), acc[:, : (N // P) * width])
-            queue.dma_start(out_view[:, :, first + lo : first + lo + width], res[:])
+            res = tile([P, N // P, PIECE], F32, "res%d" % piece)
+            evacuate(res[:].rearrange("p b s -> p (b s)"), acc[:, : (N // P) * PIECE])
+            nc.sync.dma_start(out_view[:, :, cols], res[:])
 
-        hid = tile([P, PACK, S], BF16, "hid", "num3")
+        hid = tile([P, PACK, S], BF16, "hid", "num%d" % LAST)
         for h in range(2):
-            cols = slice(h * HALF, (h + 1) * HALF)
+            cols = halves[h]
             for t in range(PACK):
                 nc.vector.scalar_tensor_tensor(
-                    hid[:, t, cols], mix[t][:, cols], unit5[:, t : t + 1], spawn[t][:, cols], ALU.mult, ALU.mult
+                    hid[:, t, cols], mix[t][:, cols], row_factor[:, t : t + 1], spawn[t][:, cols], ALU.mult, ALU.mult
                 )
             if h == 0:
-                last_layer(0, hid, 0, 0, HALF // 2, nc.scalar.copy, nc.scalar.copy, nc.sync)
-                last_layer(1, hid, 0, HALF // 2, HALF // 2, nc.scalar.copy, nc.scalar.copy, nc.sync)
+                last_layer(0, hid, nc.scalar.copy, nc.scalar.copy)
+                last_layer(1, hid, nc.scalar.copy, nc.scalar.copy)
             else:
-                last_layer(2, hid, HALF, 0, HALF // 2, nc.vector.tensor_copy, nc.scalar.copy, nc.sync)
-                last_layer(3, hid, HALF, HALF // 2, HALF // 2, nc.scalar.copy, nc.vector.tensor_copy, nc.sync)
+                last_layer(2, hid, nc.vector.tensor_copy, nc.scalar.copy)
+                last_layer(3, hid, nc.scalar.copy, nc.vector.tensor_copy)

from contextlib import ExitStack

import concourse.mybir as mybir
from concourse.masks import make_identity

K, T, S, D, N, H = 512, 2048, 512, 4, 256, 512
FLOPS = 2 * K * H * S * 2 + 2 * H * N * S

F32 = mybir.dt.float32
BF16 = mybir.dt.bfloat16
I32 = mybir.dt.int32
U32 = mybir.dt.uint32
U16 = mybir.dt.uint16
U8 = mybir.dt.uint8
FP8X4 = mybir.dt.float8_e4m3fn_x4
ALU = mybir.AluOpType
ACT = mybir.ActivationFunctionType

P = 128
PACK = 4
LIST_ROWS = 16
SCALE_ROWS = 4
HALF = S // 2
PIECE = S // 4
GROUPS = S // D
LAST = PACK - 1
LN_FLOOR = 2.0**-60
CLUTTER = 0.3
UPD_SCALE = 0.8 / 0.2
VECTOR_SQUARES = 2


def tile_picked_ygmphd_mean_p_kernel(
    tc, x_words, x_scales, w1, w2, meas, unit, w3, offs, brn, out
):
    nc = tc.nc
    halves = [slice(h * HALF, (h + 1) * HALF) for h in range(2)]
    with ExitStack() as ctx:
        sb = ctx.enter_context(tc.tile_pool(name="sb", bufs=1))
        ps = ctx.enter_context(tc.psum_pool(name="ps", bufs=1))

        def tile(shape, dtype, name, tag=None):
            return sb.tile(shape, dtype, name=name, tag=tag or name, align_bytes=64)

        def bank(name, tag):
            return ps.tile([P, S], F32, name=name, tag=tag)

        offs_sb = sb.tile([P, S // LIST_ROWS], U16, name="offs_sb")
        nc.sync.dma_start(offs_sb[:], offs)
        xs_table = tile([P, T], U8, "xs_table")
        nc.vector.memset(xs_table[:].bitcast(I32), 0)
        for q in range(P // 32):
            nc.sync.dma_start(
                xs_table[32 * q : 32 * q + SCALE_ROWS, :].bitcast(I32),
                x_scales[0, SCALE_ROWS * q : SCALE_ROWS * (q + 1), :].bitcast(I32),
            )
        xw_table = tile([P, T], U32, "xw_table")
        nc.sync.dma_start(xw_table[:].bitcast(I32), x_words[0].rearrange("p n r -> p (n r)").bitcast(I32))

        def load_halves(w, name):
            rows = w.rearrange("(p j) c -> p j c", j=PACK)
            raws = []
            for h in range(2):
                raw = tile([P, PACK, H // 2], F32, "%s_raw%d" % (name, h))
                nc.sync.dma_start(raw[:], rows[:, :, h * (H // 2) : (h + 1) * (H // 2)])
                raws.append(raw)
            return raws

        w2_raw = load_halves(w2, "w2")
        w1_raw = load_halves(w1, "w1")
        meas_sb = []
        for t in range(PACK):
            meas_t = tile([P, S], F32, "meas%d" % t)
            nc.sync.dma_start(meas_t[:], meas.rearrange("(p t) s -> p t s", t=PACK)[:, t, :])
            meas_sb.append(meas_t)
        w3_raw = tile([P, PACK, N], F32, "w3_raw")
        nc.sync.dma_start(w3_raw[:], w3.rearrange("(p j) c -> p j c", j=PACK))
        brn_sb = sb.tile([P, S // LIST_ROWS], U16, name="brn_sb")
        nc.sync.dma_start(brn_sb[:], brn)
        unit_sb = tile([P, PACK], F32, "unit_sb")
        nc.sync.dma_start(unit_sb[:], unit.rearrange("(p t) o -> p (t o)", t=PACK))

        ident = tile([P, P], F32, "ident")
        make_identity(nc, ident[:])
        ones = tile([P, 1], F32, "ones")
        nc.gpsimd.memset(ones[:], 1.0)
        clutter = tile([P, 1], F32, "clutter")
        nc.gpsimd.tensor_scalar(clutter[:], ones[:], CLUTTER, None, ALU.mult)

        warm = tile([P, 1], F32, "warm")
        nc.scalar.activation(warm[:], ones[:], ACT.Sigmoid)

        x_sc = tile([P, S], U8, "x_sc")
        nc.vector.tensor_copy(x_sc[:], xs_table[:].indirect(offs_sb[:]))
        x_q = tile([P, S], U32, "x_q")
        nc.vector.tensor_copy(x_q[:], xw_table[:].indirect(offs_sb[:]))

        def first_layer(raws, name, casts):
            dealt = tile([P, PACK, P, PACK], BF16, name + "_bf", "w_bf")
            for h in range(2):
                casts[h](
                    dealt[:, :, h * (P // 2) : (h + 1) * (P // 2), :].rearrange("p t m j -> p m j t"),
                    raws[h][:].rearrange("p j (m t) -> p m j t", t=PACK),
                )
            planes = []
            for t in range(PACK):
                codes = tile([P, P], U32, "%s_q%d" % (name, t))
                scales = tile([P, P], U8, "%s_s%d" % (name, t))
                nc.vector.quantize_mx(codes[:].bitcast(FP8X4), scales[:], dealt[:, t].rearrange("p m j -> p (m j)"))
                acc = bank("%s_acc%d" % (name, t), "%s_bank%d" % (name, t))
                nc.tensor.matmul_mx(
                    acc[:], lhsT=codes[:].bitcast(FP8X4), lhsT_scale=scales[:],
                    rhs=x_q[:].bitcast(FP8X4), rhs_scale=x_sc[:], start=True, stop=True,
                )
                planes.append(acc)
            return planes

        wg = first_layer(w2_raw, "w2", (nc.scalar.copy, nc.vector.tensor_copy))
        sig = tile([P, PACK, S], F32, "sig")
        for t in range(PACK):
            nc.scalar.activation(sig[:, t, :], wg[t][:], ACT.Sigmoid, scale=-1.0)
        lnsig = tile([P, PACK, S], F32, "lnsig")
        nc.scalar.activation(lnsig[:], sig[:], ACT.Ln, bias=LN_FLOOR)

        mu = first_layer(w1_raw, "w1", (nc.vector.tensor_copy, nc.vector.tensor_copy))
        diff = []
        for t in range(PACK):
            diff_t = tile([P, S], F32, "diff%d" % t)
            nc.vector.tensor_tensor(diff_t[:], mu[t][:], meas_sb[t][:], ALU.subtract)
            diff.append(diff_t)
        wei = []
        for t in range(PACK):
            wei_t = tile([P, S], F32, "wei%d" % t)
            nc.vector.scalar_tensor_tensor(wei_t[:], lnsig[:, t, :], -1.0, wg[t][:], ALU.mult, ALU.max)
            wei.append(wei_t)

        w3_bf = tile([P, N, PACK], BF16, "w3_bf")
        nc.vector.tensor_copy(
            w3_bf[:].rearrange("p (c i) j -> p c j i", i=4), w3_raw[:].rearrange("p j (c i) -> p c j i", i=4)
        )
        w3_q = tile([P, N], U32, "w3_q")
        w3_s = tile([P, N], U8, "w3_s")
        nc.vector.quantize_mx(w3_q[:].bitcast(FP8X4), w3_s[:], w3_bf[:].rearrange("p c j -> p (c j)"))
        row_factor = tile([P, PACK], F32, "row_factor")
        nc.vector.tensor_scalar(row_factor[:], unit_sb[:], 0.2, None, ALU.mult)

        lik = []
        for t in range(PACK):
            tanh_t = sig[:, t % 2, :]
            nc.scalar.activation(tanh_t, diff[t][:], ACT.Tanh)
            square = tile([P, S], F32, "square%d" % t)
            if t < VECTOR_SQUARES:
                nc.vector.tensor_tensor(square[:], tanh_t, tanh_t, ALU.mult)
            else:
                nc.scalar.activation(square[:], tanh_t, ACT.Square)
            lik_t = tile([P, S], F32, "lik%d" % t)
            nc.scalar.activation(lik_t[:], square[:], ACT.Exp, scale=-1.5)
            lik.append(lik_t)

        upd, picked = [], []
        for t in range(PACK):
            num = tile([P, S], F32, "num%d" % t, "num%d" % (0 if t == 2 else t))
            if t == LAST:
                for cols in halves:
                    nc.gpsimd.tensor_tensor(num[:, cols], wei[t][:, cols], lik[t][:, cols], ALU.mult)
            else:
                nc.vector.tensor_tensor(num[:], wei[t][:], lik[t][:], ALU.mult)
            members = num[:].rearrange("p (v d) -> p v d", d=D)
            if t == 0:
                pairs = tile([P, GROUPS, 2], F32, "pairs")
                nc.vector.tensor_tensor(pairs[:], members[:, :, 0:2], members[:, :, 2:4], ALU.add)
                den = tile([P, GROUPS], F32, "den")
                nc.vector.scalar_tensor_tensor(den[:], pairs[:, :, 0], CLUTTER, pairs[:, :, 1], ALU.add, ALU.add)
                rden = tile([P, GROUPS], F32, "rden0")
                nc.vector.reciprocal(rden[:], den[:])
            else:
                den_turned = bank("den_turned%d" % t, "w2_bank%d" % t)
                nc.tensor.matmul(
                    den_turned[:, :P], lhsT=clutter[:].to_broadcast([P, GROUPS]), rhs=ident[:],
                    is_transpose=True, start=True, stop=False,
                )
                for d in range(D):
                    nc.tensor.matmul(
                        den_turned[:, :P], lhsT=members[:, :, d], rhs=ident[:],
                        is_transpose=True, start=False, stop=(d == D - 1),
                    )
                rden_turned = tile([P, P], F32, "rden_turned%d" % t)
                nc.vector.reciprocal(rden_turned[:], den_turned[:, :P])
                rden = bank("rden%d" % t, "w2_bank%d" % t)
                nc.tensor.transpose(rden[:, :GROUPS], rden_turned[:], ident[:])
            upd_t = tile([P, S], F32, "upd%d" % t)
            nc.vector.scalar_tensor_tensor(
                upd_t[:].rearrange("p (v d) -> p v d", d=D),
                members,
                UPD_SCALE,
                rden[:, :GROUPS].unsqueeze(2).to_broadcast([P, GROUPS, D]),
                ALU.mult, ALU.mult,
            )
            picked_t = tile([P, S], F32, "picked%d" % t)
            for h in range(2):
                offsets = brn_sb[:, h * (HALF // LIST_ROWS) : (h + 1) * (HALF // LIST_ROWS)]
                nc.scalar.activation(picked_t[:, halves[h]], upd_t[:].indirect(offsets), ACT.Copy)
            picked.append(picked_t)
            upd.append(upd_t)

        mix = []
        for t in range(PACK):
            mix_t = tile([P, S], F32, "mix%d" % t, "lik%d" % (LAST - t))
            for cols in halves:
                nc.gpsimd.tensor_tensor(mix_t[:, cols], wei[t][:, cols], upd[t][:, cols], ALU.add)
            mix.append(mix_t)
        spawn = []
        for t in range(PACK):
            spawn_t = tile([P, S], F32, "spawn%d" % t)
            nc.vector.scalar_tensor_tensor(spawn_t[:], picked[t][:], 0.7 / UPD_SCALE, mu[t][:], ALU.mult, ALU.add)
            spawn.append(spawn_t)

        out_view = out.rearrange("(b p) s -> p b s", p=P)

        def last_layer(piece, hid, interleave, evacuate):
            cols = slice(piece * PIECE, (piece + 1) * PIECE)
            packed = tile([P, PIECE, PACK], BF16, "packed%d" % piece)
            interleave(
                packed[:].rearrange("p (c i) t -> p c t i", i=4), hid[:, :, cols].rearrange("p t (c i) -> p c t i", i=4)
            )
            hid_q = tile([P, PIECE], U32, "hid_q%d" % piece)
            hid_s = tile([P, PIECE], U8, "hid_s%d" % piece)
            nc.vector.quantize_mx(hid_q[:].bitcast(FP8X4), hid_s[:], packed[:].rearrange("p c t -> p (c t)"))
            acc = bank("out_acc%d" % piece, "w2_bank%d" % piece)
            for b in range(N // P):
                nc.tensor.matmul_mx(
                    acc[:, b * PIECE : (b + 1) * PIECE],
                    lhsT=w3_q[:, b * P : (b + 1) * P].bitcast(FP8X4), lhsT_scale=w3_s[:, b * P : (b + 1) * P],
                    rhs=hid_q[:].bitcast(FP8X4), rhs_scale=hid_s[:], start=True, stop=True,
                )
            res = tile([P, N // P, PIECE], F32, "res%d" % piece)
            evacuate(res[:].rearrange("p b s -> p (b s)"), acc[:, : (N // P) * PIECE])
            nc.sync.dma_start(out_view[:, :, cols], res[:])

        hid = tile([P, PACK, S], BF16, "hid", "num%d" % LAST)
        for h in range(2):
            cols = halves[h]
            for t in range(PACK):
                nc.vector.scalar_tensor_tensor(
                    hid[:, t, cols], mix[t][:, cols], row_factor[:, t : t + 1], spawn[t][:, cols], ALU.mult, ALU.mult
                )
            if h == 0:
                last_layer(0, hid, nc.scalar.copy, nc.scalar.copy)
                last_layer(1, hid, nc.scalar.copy, nc.scalar.copy)
            else:
                last_layer(2, hid, nc.vector.tensor_copy, nc.scalar.copy)
                last_layer(3, hid, nc.scalar.copy, nc.vector.tensor_copy)
